import numpy as np
import ml_dtypes


def mxq(x, axis, fmt="e4m3"):
    dtype, down = {"e4m3": (ml_dtypes.float8_e4m3fn, 7), "e5m2": (ml_dtypes.float8_e5m2, 14)}[fmt]
    v = np.moveaxis(np.asarray(x, np.float32).astype(ml_dtypes.bfloat16).astype(np.float64), axis, -1)
    blocks = v.reshape(v.shape[:-1] + (-1, 32))
    amax = np.abs(blocks).max(-1, keepdims=True)
    byte = np.maximum(np.where(amax > 0, np.frexp(amax)[1] - 1 + 127, 0) - down, 1)
    scale = np.exp2(byte - 127.0)
    codes = (blocks / scale).astype(np.float32).astype(dtype).astype(np.float64)
    return np.moveaxis((codes * scale).reshape(v.shape), -1, axis)


WIDE = False


def mx_kscale(k):
    if not WIDE:
        return np.ones(k)
    levels = np.array([10, -10, 5, -5, 0])
    if k % 512:
        return np.exp2(np.random.permutation(np.resize(levels, k // 32))).repeat(32)
    a = np.empty((k // 512, 16))
    for p in range(k // 512):
        a[p, :8] = np.random.permutation(np.resize(levels, 8))
        for g in range(8):
            far = levels[np.abs(levels - a[p, g]) >= 10]
            a[p, g + 8] = far[np.random.randint(len(far))]
    return np.exp2(a.ravel()).repeat(32)


def f64(x):
    return np.asarray(x).astype(np.float64)


def striped(idx):
    return np.tile(np.asarray(idx).reshape(-1, 16).T, (8, 1)).astype(np.uint16)


def unstriped(offs):
    return offs[:16].T.reshape(-1).astype(np.int64)


E2M1 = np.array([0.0, 0.5, 1.0, 1.5, 2.0, 3.0, 4.0, 6.0, -0.0, -0.5, -1.0, -1.5, -2.0, -3.0, -4.0, -6.0])


def pack_weight(w, fmt):
    k, n = w.shape
    w = f64(np.asarray(w, np.float32).astype(ml_dtypes.bfloat16)).reshape(k // 32, 32, n)
    amax = np.abs(w).max(1)
    if fmt == "e4m3":
        byte = np.frexp(amax)[1] - 1 + 127 - 7
    else:
        mant, ex = np.frexp(amax / 6.0)
        byte = np.where(mant > 0.5, ex, ex - 1) + 127
    byte = np.clip(np.where(amax > 0, byte, 1), 1, 254)
    scaled = (w * np.exp2(127.0 - byte)[:, None, :]).reshape(k, n).astype(np.float32)
    by_word = np.ascontiguousarray(scaled.reshape(k // 512, 128, 4, n).transpose(0, 1, 3, 2))
    if fmt == "e4m3":
        words = by_word.astype(ml_dtypes.float8_e4m3fn).view(np.uint8)
    else:
        c = by_word.astype(ml_dtypes.float4_e2m1fn).view(np.uint8) & 0xF
        words = (c[..., 0::2] | (c[..., 1::2] << 4)).reshape(k // 512, 128, 2 * n)
    return np.ascontiguousarray(words), np.ascontiguousarray(byte.astype(np.uint8).reshape(k // 512, 16, n))


def unpack_weight(words, scales, fmt):
    g, _, n = scales.shape
    words = np.ascontiguousarray(words).reshape(g, 128, n, -1)
    if fmt == "e4m3":
        vals = words.view(ml_dtypes.float8_e4m3fn).astype(np.float64)
    else:
        nib = np.empty((g, 128, n, 4), np.uint8)
        nib[..., 0::2] = words & 0xF
        nib[..., 1::2] = words >> 4
        vals = E2M1[nib]
    vals = vals * np.repeat(np.exp2(scales.astype(np.float64) - 127.0), 8, axis=1)[..., None]
    return vals.transpose(0, 1, 3, 2).reshape(g * 512, n)


def bf(x):
    return np.asarray(x, np.float32).astype(ml_dtypes.bfloat16)


def planes(Y):
    r, m = Y.shape
    b = f64(bf(Y)).reshape(r // 32, 32, m)
    amax = np.abs(b).max(1)
    byte = np.clip(np.where(amax > 0, np.frexp(amax)[1] - 1 + 127 - 7, 1), 1, 254)
    codes = (b * np.exp2(127.0 - byte)[:, None, :]).reshape(r, m).astype(np.float32).astype(ml_dtypes.float8_e4m3fn).view(np.uint8)
    words = codes.reshape(r // 512, 128, 4, m).transpose(0, 1, 3, 2)
    return np.ascontiguousarray(words), np.ascontiguousarray(byte.astype(np.uint8).reshape(r // 512, 16, m))


D, T, I, Q = 512, 4096, 1024, 512


def setup_inputs():
    n = np.random.standard_normal
    idx = np.random.permutation(T)[:I]
    fd = mx_kscale(D)
    vocp = pack_weight(n((D, T)) / fd[:, None], "e4m3")
    return {
        "hid": (n((D, Q)) * 1.0 / np.sqrt(D) * fd[:, None]).astype(np.float32),
        "voc_words": vocp[0],
        "voc_scales": vocp[1],
        "offs": striped(idx),
    }


def reference(hid, voc_words, voc_scales, offs):
    idx = unstriped(offs)
    vocu = unpack_weight(voc_words, voc_scales, "e4m3")
    hidq = mxq(f64(hid), 0, "e4m3")
    vocidxg = vocu[:, idx]
    a = hidq.T @ vocidxg
    p = np.exp(a)
    z = np.sum(p, axis=1, keepdims=True)
    lp = a - np.log(z)
    n = np.sum(p * lp, axis=1, keepdims=True) / z
    y = np.abs(n - lp)
    words, scales = planes(y)
    return y, words, scales

@@ -1,0 +1,161 @@
+from contextlib import ExitStack
+
+import concourse.mybir as mybir
+
+D, T, I, Q = 512, 4096, 1024, 512
+FLOPS = 2 * D * I * Q
+
+F32 = mybir.dt.float32
+BF16 = mybir.dt.bfloat16
+I32 = mybir.dt.int32
+U32 = mybir.dt.uint32
+U16 = mybir.dt.uint16
+U8 = mybir.dt.uint8
+FP8X4 = mybir.dt.float8_e4m3fn_x4
+ALU = mybir.AluOpType
+ACT = mybir.ActivationFunctionType
+
+P = 128
+PACK = 4
+BANK = 512
+HALVES = I // BANK
+QUARTER = 256
+
+
+def tile_attend_typical_pl_kernel(tc, hid, voc_words, voc_scales, offs, out_0, out_1, out_2):
+    nc = tc.nc
+    with ExitStack() as ctx:
+        sb = ctx.enter_context(tc.tile_pool(name="sb", bufs=1))
+        psum = ctx.enter_context(tc.psum_pool(name="psum", bufs=1))
+
+        offsets = sb.tile([P, I // 16], U16, name="offsets")
+        words = sb.tile([P, T], U32, name="words", align_bytes=64)
+        scale_rows = sb.tile([P, T], U8, name="scale_rows", align_bytes=64)
+        hid_raw = sb.tile([P, PACK, Q], F32, name="hid_raw", align_bytes=64)
+        picked_rows = sb.tile([P, I], U8, name="picked_rows", align_bytes=64)
+        voc_plane = sb.tile([P, I], U8, name="voc_plane", align_bytes=64)
+
+        nc.vector.memset(scale_rows[0:P - 16, :].bitcast(I32), 0)
+        nc.vector.memset(voc_plane[:].bitcast(I32), 0)
+        nc.sync.dma_start(offsets[:], offs)
+        nc.sync.dma_start(words[:].bitcast(I32), voc_words[0].rearrange("p t r -> p (t r)").bitcast(I32))
+        nc.scalar.dma_start(scale_rows[P - 16:P, :].bitcast(I32), voc_scales[0].bitcast(I32))
+        nc.sync.dma_start(hid_raw[:], hid.rearrange("(p j) q -> p j q", j=PACK))
+
+        nc.vector.tensor_copy(picked_rows[:], scale_rows[:].indirect(offsets[:]))
+        for quad in range(4):
+            first = P - 16 + 4 * quad
+            nc.scalar.dma_start(voc_plane[32 * quad:32 * quad + 4, :].bitcast(I32),
+                                picked_rows[first:first + 4, :].bitcast(I32))
+
+        picked_words = []
+        for h in range(HALVES):
+            half_words = sb.tile([P, BANK], U32, name=f"picked_words{h}", align_bytes=64)
+            nc.vector.tensor_copy(half_words[:], words[:].indirect(offsets[:, h * 32:(h + 1) * 32]))
+            picked_words.append(half_words)
+
+        hid_by_row = hid_raw[:].rearrange("p j (s r) -> p s j r", r=PACK)
+        hid_codes, hid_scales = [], []
+        for pair in range(2):
+            dealt = sb.tile([P, 2, P, PACK], BF16, name=f"dealt{pair}", tag=f"staging{pair}", align_bytes=64)
+            source = hid_by_row[:, :, :, 2 * pair:2 * pair + 2]
+            target = dealt[:].rearrange("p r s j -> p s j r")
+            if pair == 0:
+                nc.vector.tensor_copy(target, source)
+            else:
+                nc.scalar.copy(target, source)
+            for r in range(2):
+                codes = sb.tile([P, P], U32, name=f"hid_codes{pair}{r}", align_bytes=64)
+                scales = sb.tile([P, P], U8, name=f"hid_scales{pair}{r}", align_bytes=64)
+                nc.vector.quantize_mx(codes[:].bitcast(FP8X4), scales[:], dealt[:, r].rearrange("p s j -> p (s j)"))
+                hid_codes.append(codes)
+                hid_scales.append(scales)
+
+        y = sb.tile([P, PACK, I], F32, name="y", align_bytes=64)
+        out_rows = out_0.rearrange("(p r) i -> p r i", r=PACK)
+        neg_a, least, prob, inv_z, neg_mean = {}, {}, {}, {}, {}
+
+        def scores(r, h):
+            if h == 0:
+                tag = "staging1" if r == 1 else f"neg_a{r}"
+                neg_a[r] = sb.tile([P, I], F32, name=f"neg_a{r}", tag=tag, align_bytes=64)
+            bank = psum.tile([P, BANK], F32, name=f"bank{r}{h}")
+            cols = slice(h * BANK, (h + 1) * BANK)
+            nc.tensor.matmul_mx(bank[:], lhsT=hid_codes[r][:].bitcast(FP8X4), lhsT_scale=hid_scales[r][:],
+                                rhs=picked_words[h][:].bitcast(FP8X4), rhs_scale=voc_plane[:, cols],
+                                start=True, stop=True)
+            low = sb.tile([P, 1], F32, name=f"least{r}{h}")
+            nc.vector.tensor_scalar(neg_a[r][:, cols], bank[:], -1.0, least[r][:] if h else None,
+                                    ALU.mult, ALU.min, accum_out=low[:])
+            least[r] = low
+
+        def weights(r):
+            prob[r] = sb.tile([P, I], F32, name=f"p{r}", align_bytes=64)
+            z = sb.tile([P, 1], F32, name=f"z{r}")
+            nc.scalar.activation(prob[r][:], neg_a[r][:], ACT.Exp, bias=least[r][:], scale=-1.0, accum_out=z[:])
+            inv_z[r] = sb.tile([P, 1], F32, name=f"inv_z{r}")
+            nc.vector.reciprocal(inv_z[r][:], z[:])
+
+        def mean(r):
+            neg_mean[r] = sb.tile([P, 1], F32, name=f"neg_mean{r}")
+            nc.vector.scalar_tensor_tensor(prob[r][:], neg_a[r][:], inv_z[r][:], prob[r][:], ALU.mult, ALU.mult,
+                                           accum_out=neg_mean[r][:])
+
+        def distance(r, cols):
+            nc.scalar.activation(y[:, r, cols], neg_a[r][:, cols], ACT.Abs, bias=neg_mean[r][:], scale=-1.0)
+
+        def store(rows, cols):
+            nc.sync.dma_start(out_rows[:, rows, cols], y[:, rows, cols])
+
+        first_half, second_half = slice(0, BANK), slice(BANK, I)
+        scores(0, 0)
+        scores(1, 0)
+        scores(0, 1)
+        weights(0)
+        scores(1, 1)
+        weights(1)
+        scores(2, 0)
+        scores(3, 0)
+        scores(2, 1)
+        weights(2)
+        mean(0)
+        distance(0, slice(0, I))
+        store(0, slice(0, I))
+        mean(1)
+        distance(1, first_half)
+        store(1, first_half)
+        scores(3, 1)
+        weights(3)
+        distance(1, second_half)
+        store(1, second_half)
+        mean(2)
+        mean(3)
+
+        y_codes = sb.tile([P, I], U32, name="y_codes", align_bytes=64)
+        y_scales = sb.tile([P, I], U8, name="y_scales", align_bytes=64)
+        words_out = out_1[0].rearrange("p c r -> p (c r)").bitcast(I32)
+        quarters = [slice(c * QUARTER, (c + 1) * QUARTER) for c in range(I // QUARTER)]
+        for r in (2, 3):
+            distance(r, quarters[0])
+            distance(r, quarters[1])
+            store(r, first_half)
+        for cols in quarters[2:]:
+            distance(2, cols)
+            distance(3, cols)
+            store(slice(2, 4), cols)
+        for c, cols in enumerate(quarters):
+            woven = sb.tile([P, QUARTER, PACK], BF16, name=f"woven{c}", align_bytes=64)
+            source = y[:, :, cols].rearrange("p r (c i) -> p c r i", i=4)
+            target = woven[:].rearrange("p (c i) r -> p c r i", i=4)
+            if c == I // QUARTER - 1:
+                nc.scalar.copy(target, source)
+            else:
+                nc.vector.tensor_copy(target, source)
+            nc.vector.quantize_mx(y_codes[:, cols].bitcast(FP8X4), y_scales[:, cols],
+                                  woven[:].rearrange("p c r -> p (c r)"))
+            nc.sync.dma_start(words_out[:, cols], y_codes[:, cols].bitcast(I32))
+
+        for quad in range(4):
+            engine = nc.scalar if quad % 2 == 0 else nc.sync
+            engine.dma_start(out_2[0, 4 * quad:4 * quad + 4, :].bitcast(I32),
+                             y_scales[32 * quad:32 * quad + 4, :].bitcast(I32))

@@ -73,18 +73,19 @@ def tile_attend_typical_pl_kernel(tc, hid, voc_words, voc_scales, offs, out_0, o
 
         y = sb.tile([P, PACK, I], F32, name="y", align_bytes=64)
         out_rows = out_0.rearrange("(p r) i -> p r i", r=PACK)
-        neg_a, least, prob, inv_z, neg_mean = {}, {}, {}, {}, {}
+        neg_a, least, prob, inv_z, neg_mean, banks = {}, {}, {}, {}, {}, {}
 
         def scores(r, h):
             if h == 0:
-                tag = "staging1" if r == 1 else f"neg_a{r}"
-                neg_a[r] = sb.tile([P, I], F32, name=f"neg_a{r}", tag=tag, align_bytes=64)
+                neg_a[r] = sb.tile([P, I], F32, name=f"neg_a{r}", align_bytes=64)
             bank = psum.tile([P, BANK], F32, name=f"bank{r}{h}")
             cols = slice(h * BANK, (h + 1) * BANK)
             nc.tensor.matmul_mx(bank[:], lhsT=hid_codes[r][:].bitcast(FP8X4), lhsT_scale=hid_scales[r][:],
                                 rhs=picked_words[h][:].bitcast(FP8X4), rhs_scale=voc_plane[:, cols],
                                 start=True, stop=True)
-            low = sb.tile([P, 1], F32, name=f"least{r}{h}")
+            banks[r, h] = bank
+            tag = "staging1" if (r, h) == (1, 1) else f"least{r}{h}"
+            low = sb.tile([P, 1], F32, name=f"least{r}{h}", tag=tag, align_bytes=64)
             nc.vector.tensor_scalar(neg_a[r][:, cols], bank[:], -1.0, least[r][:] if h else None,
                                     ALU.mult, ALU.min, accum_out=low[:])
             least[r] = low
@@ -98,8 +99,12 @@ def tile_attend_typical_pl_kernel(tc, hid, voc_words, voc_scales, offs, out_0, o
 
         def mean(r):
             neg_mean[r] = sb.tile([P, 1], F32, name=f"neg_mean{r}")
-            nc.vector.scalar_tensor_tensor(prob[r][:], neg_a[r][:], inv_z[r][:], prob[r][:], ALU.mult, ALU.mult,
-                                           accum_out=neg_mean[r][:])
+            sums = sb.tile([P, HALVES], F32, name=f"sums{r}")
+            for h in range(HALVES):
+                cols = slice(h * BANK, (h + 1) * BANK)
+                nc.vector.scalar_tensor_tensor(prob[r][:, cols], banks[r, h][:], -1.0, prob[r][:, cols],
+                                               ALU.mult, ALU.mult, accum_out=sums[:, h:h + 1])
+            nc.vector.tensor_scalar(neg_mean[r][:], sums[:, 0:1], sums[:, 1:2], inv_z[r][:], ALU.add, ALU.mult)
 
         def distance(r, cols):
             nc.scalar.activation(y[:, r, cols], neg_a[r][:, cols], ACT.Abs, bias=neg_mean[r][:], scale=-1.0)
@@ -145,8 +150,8 @@ def tile_attend_typical_pl_kernel(tc, hid, voc_words, voc_scales, offs, out_0, o
             store(slice(2, 4), cols)
         for c, cols in enumerate(quarters):
             woven = sb.tile([P, QUARTER, PACK], BF16, name=f"woven{c}", align_bytes=64)
-            source = y[:, :, cols].rearrange("p r (c i) -> p c r i", i=4)
-            target = woven[:].rearrange("p (c i) r -> p c r i", i=4)
+            source = y[:, :, cols].rearrange("p r (c i) -> p c r i", i=2)
+            target = woven[:].rearrange("p (c i) r -> p c r i", i=2)
             if c == I // QUARTER - 1:
                 nc.scalar.copy(target, source)
             else:

@@ -20,6 +20,8 @@ PACK = 4
 BANK = 512
 HALVES = I // BANK
 QUARTER = 256
+VECTOR_ROWS = 84
+VECTOR_WEAVE = 704
 
 
 def tile_attend_typical_pl_kernel(tc, hid, voc_words, voc_scales, offs, out_0, out_1, out_2):
@@ -61,7 +63,8 @@ def tile_attend_typical_pl_kernel(tc, hid, voc_words, voc_scales, offs, out_0, o
             source = hid_by_row[:, :, :, 2 * pair:2 * pair + 2]
             target = dealt[:].rearrange("p r s j -> p s j r")
             if pair == 0:
-                nc.vector.tensor_copy(target, source)
+                nc.vector.tensor_copy(target[:, :VECTOR_ROWS], source[:, :VECTOR_ROWS])
+                nc.scalar.copy(target[:, VECTOR_ROWS:], source[:, VECTOR_ROWS:])
             else:
                 nc.scalar.copy(target, source)
             for r in range(2):
@@ -73,7 +76,7 @@ def tile_attend_typical_pl_kernel(tc, hid, voc_words, voc_scales, offs, out_0, o
 
         y = sb.tile([P, PACK, I], F32, name="y", align_bytes=64)
         out_rows = out_0.rearrange("(p r) i -> p r i", r=PACK)
-        neg_a, least, prob, inv_z, neg_mean, banks = {}, {}, {}, {}, {}, {}
+        neg_a, least, prob, inv_z, neg_mean, banks, sums = {}, {}, {}, {}, {}, {}, {}
 
         def scores(r, h):
             if h == 0:
@@ -84,7 +87,7 @@ def tile_attend_typical_pl_kernel(tc, hid, voc_words, voc_scales, offs, out_0, o
                                 rhs=picked_words[h][:].bitcast(FP8X4), rhs_scale=voc_plane[:, cols],
                                 start=True, stop=True)
             banks[r, h] = bank
-            tag = "staging1" if (r, h) == (1, 1) else f"least{r}{h}"
+            tag = "staging1" if (r, h) == (1, 0) else f"least{r}{h}"
             low = sb.tile([P, 1], F32, name=f"least{r}{h}", tag=tag, align_bytes=64)
             nc.vector.tensor_scalar(neg_a[r][:, cols], bank[:], -1.0, least[r][:] if h else None,
                                     ALU.mult, ALU.min, accum_out=low[:])
@@ -97,14 +100,17 @@ def tile_attend_typical_pl_kernel(tc, hid, voc_words, voc_scales, offs, out_0, o
             inv_z[r] = sb.tile([P, 1], F32, name=f"inv_z{r}")
             nc.vector.reciprocal(inv_z[r][:], z[:])
 
+        def weighted_sum(r, h):
+            if h == 0:
+                sums[r] = sb.tile([P, HALVES], F32, name=f"sums{r}")
+            cols = slice(h * BANK, (h + 1) * BANK)
+            nc.vector.scalar_tensor_tensor(prob[r][:, cols], banks[r, h][:], -1.0, prob[r][:, cols],
+                                           ALU.mult, ALU.mult, accum_out=sums[r][:, h:h + 1])
+
         def mean(r):
             neg_mean[r] = sb.tile([P, 1], F32, name=f"neg_mean{r}")
-            sums = sb.tile([P, HALVES], F32, name=f"sums{r}")
-            for h in range(HALVES):
-                cols = slice(h * BANK, (h + 1) * BANK)
-                nc.vector.scalar_tensor_tensor(prob[r][:, cols], banks[r, h][:], -1.0, prob[r][:, cols],
-                                               ALU.mult, ALU.mult, accum_out=sums[:, h:h + 1])
-            nc.vector.tensor_scalar(neg_mean[r][:], sums[:, 0:1], sums[:, 1:2], inv_z[r][:], ALU.add, ALU.mult)
+            nc.vector.tensor_scalar(neg_mean[r][:], sums[r][:, 0:1], sums[r][:, 1:2], inv_z[r][:],
+                                    ALU.add, ALU.mult)
 
         def distance(r, cols):
             nc.scalar.activation(y[:, r, cols], neg_a[r][:, cols], ACT.Abs, bias=neg_mean[r][:], scale=-1.0)
@@ -112,53 +118,71 @@ def tile_attend_typical_pl_kernel(tc, hid, voc_words, voc_scales, offs, out_0, o
         def store(rows, cols):
             nc.sync.dma_start(out_rows[:, rows, cols], y[:, rows, cols])
 
-        first_half, second_half = slice(0, BANK), slice(BANK, I)
+        halves = [slice(h * BANK, (h + 1) * BANK) for h in range(HALVES)]
+
+        def distances(r):
+            for cols in halves:
+                distance(r, cols)
+                store(r, cols)
+
         scores(0, 0)
-        scores(1, 0)
         scores(0, 1)
         weights(0)
+        scores(1, 0)
+        scores(2, 0)
         scores(1, 1)
         weights(1)
-        scores(2, 0)
-        scores(3, 0)
         scores(2, 1)
         weights(2)
+        weighted_sum(0, 0)
+        weighted_sum(0, 1)
+        scores(3, 0)
         mean(0)
-        distance(0, slice(0, I))
-        store(0, slice(0, I))
-        mean(1)
-        distance(1, first_half)
-        store(1, first_half)
+        distances(0)
+        weighted_sum(1, 0)
         scores(3, 1)
         weights(3)
-        distance(1, second_half)
-        store(1, second_half)
+        weighted_sum(1, 1)
+        weighted_sum(2, 0)
+        mean(1)
+        distances(1)
+        weighted_sum(2, 1)
+        weighted_sum(3, 0)
         mean(2)
+        weighted_sum(3, 1)
         mean(3)
 
         y_codes = sb.tile([P, I], U32, name="y_codes", align_bytes=64)
         y_scales = sb.tile([P, I], U8, name="y_scales", align_bytes=64)
         words_out = out_1[0].rearrange("p c r -> p (c r)").bitcast(I32)
         quarters = [slice(c * QUARTER, (c + 1) * QUARTER) for c in range(I // QUARTER)]
-        for r in (2, 3):
-            distance(r, quarters[0])
-            distance(r, quarters[1])
-            store(r, first_half)
-        for cols in quarters[2:]:
-            distance(2, cols)
-            distance(3, cols)
-            store(slice(2, 4), cols)
-        for c, cols in enumerate(quarters):
-            woven = sb.tile([P, QUARTER, PACK], BF16, name=f"woven{c}", align_bytes=64)
-            source = y[:, :, cols].rearrange("p r (c i) -> p c r i", i=2)
-            target = woven[:].rearrange("p (c i) r -> p c r i", i=2)
-            if c == I // QUARTER - 1:
-                nc.scalar.copy(target, source)
-            else:
-                nc.vector.tensor_copy(target, source)
+        for r, c in ((2, 0), (2, 1), (2, 2), (3, 0), (3, 1), (2, 3), (3, 2), (3, 3)):
+            distance(r, quarters[c])
+            if c % 2:
+                store(r, halves[c // 2])
+        woven = {}
+
+        def weave(c):
+            woven[c] = sb.tile([P, QUARTER, PACK], BF16, name=f"woven{c}", align_bytes=64)
+            source = y[:, :, quarters[c]].rearrange("p r (c i) -> p c r i", i=2)
+            target = woven[c][:].rearrange("p (c i) r -> p c r i", i=2)
+            split = min(max(VECTOR_WEAVE - c * QUARTER, 0), QUARTER) // 2
+            if split > 0:
+                nc.vector.tensor_copy(target[:, :split], source[:, :split])
+            if split < QUARTER // 2:
+                nc.scalar.copy(target[:, split:], source[:, split:])
+
+        def quantise(c):
+            cols = quarters[c]
             nc.vector.quantize_mx(y_codes[:, cols].bitcast(FP8X4), y_scales[:, cols],
-                                  woven[:].rearrange("p c r -> p (c r)"))
+                                  woven[c][:].rearrange("p c r -> p (c r)"))
             nc.sync.dma_start(words_out[:, cols], y_codes[:, cols].bitcast(I32))
+
+        weave(0)
+        for c in range(len(quarters)):
+            if c + 1 < len(quarters):
+                weave(c + 1)
+            quantise(c)
 
         for quad in range(4):
             engine = nc.scalar if quad % 2 == 0 else nc.sync

from contextlib import ExitStack

import concourse.mybir as mybir

D, T, I, Q = 512, 4096, 1024, 512
FLOPS = 2 * D * I * Q

F32 = mybir.dt.float32
BF16 = mybir.dt.bfloat16
I32 = mybir.dt.int32
U32 = mybir.dt.uint32
U16 = mybir.dt.uint16
U8 = mybir.dt.uint8
FP8X4 = mybir.dt.float8_e4m3fn_x4
ALU = mybir.AluOpType
ACT = mybir.ActivationFunctionType

P = 128
PACK = 4
BANK = 512
HALVES = I // BANK
QUARTER = 256
VECTOR_ROWS = 84
VECTOR_WEAVE = 704


def tile_attend_typical_pl_kernel(tc, hid, voc_words, voc_scales, offs, out_0, out_1, out_2):
    nc = tc.nc
    with ExitStack() as ctx:
        sb = ctx.enter_context(tc.tile_pool(name="sb", bufs=1))
        psum = ctx.enter_context(tc.psum_pool(name="psum", bufs=1))

        offsets = sb.tile([P, I // 16], U16, name="offsets")
        words = sb.tile([P, T], U32, name="words", align_bytes=64)
        scale_rows = sb.tile([P, T], U8, name="scale_rows", align_bytes=64)
        hid_raw = sb.tile([P, PACK, Q], F32, name="hid_raw", align_bytes=64)
        picked_rows = sb.tile([P, I], U8, name="picked_rows", align_bytes=64)
        voc_plane = sb.tile([P, I], U8, name="voc_plane", align_bytes=64)

        nc.vector.memset(scale_rows[0:P - 16, :].bitcast(I32), 0)
        nc.vector.memset(voc_plane[:].bitcast(I32), 0)
        nc.sync.dma_start(offsets[:], offs)
        nc.sync.dma_start(words[:].bitcast(I32), voc_words[0].rearrange("p t r -> p (t r)").bitcast(I32))
        nc.scalar.dma_start(scale_rows[P - 16:P, :].bitcast(I32), voc_scales[0].bitcast(I32))
        nc.sync.dma_start(hid_raw[:], hid.rearrange("(p j) q -> p j q", j=PACK))

        nc.vector.tensor_copy(picked_rows[:], scale_rows[:].indirect(offsets[:]))
        for quad in range(4):
            first = P - 16 + 4 * quad
            nc.scalar.dma_start(voc_plane[32 * quad:32 * quad + 4, :].bitcast(I32),
                                picked_rows[first:first + 4, :].bitcast(I32))

        picked_words = []
        for h in range(HALVES):
            half_words = sb.tile([P, BANK], U32, name=f"picked_words{h}", align_bytes=64)
            nc.vector.tensor_copy(half_words[:], words[:].indirect(offsets[:, h * 32:(h + 1) * 32]))
            picked_words.append(half_words)

        hid_by_row = hid_raw[:].rearrange("p j (s r) -> p s j r", r=PACK)
        hid_codes, hid_scales = [], []
        for pair in range(2):
            dealt = sb.tile([P, 2, P, PACK], BF16, name=f"dealt{pair}", tag=f"staging{pair}", align_bytes=64)
            source = hid_by_row[:, :, :, 2 * pair:2 * pair + 2]
            target = dealt[:].rearrange("p r s j -> p s j r")
            if pair == 0:
                nc.vector.tensor_copy(target[:, :VECTOR_ROWS], source[:, :VECTOR_ROWS])
                nc.scalar.copy(target[:, VECTOR_ROWS:], source[:, VECTOR_ROWS:])
            else:
                nc.scalar.copy(target, source)
            for r in range(2):
                codes = sb.tile([P, P], U32, name=f"hid_codes{pair}{r}", align_bytes=64)
                scales = sb.tile([P, P], U8, name=f"hid_scales{pair}{r}", align_bytes=64)
                nc.vector.quantize_mx(codes[:].bitcast(FP8X4), scales[:], dealt[:, r].rearrange("p s j -> p (s j)"))
                hid_codes.append(codes)
                hid_scales.append(scales)

        y = sb.tile([P, PACK, I], F32, name="y", align_bytes=64)
        out_rows = out_0.rearrange("(p r) i -> p r i", r=PACK)
        neg_a, least, prob, inv_z, neg_mean, banks, sums = {}, {}, {}, {}, {}, {}, {}

        def scores(r, h):
            if h == 0:
                neg_a[r] = sb.tile([P, I], F32, name=f"neg_a{r}", align_bytes=64)
            bank = psum.tile([P, BANK], F32, name=f"bank{r}{h}")
            cols = slice(h * BANK, (h + 1) * BANK)
            nc.tensor.matmul_mx(bank[:], lhsT=hid_codes[r][:].bitcast(FP8X4), lhsT_scale=hid_scales[r][:],
                                rhs=picked_words[h][:].bitcast(FP8X4), rhs_scale=voc_plane[:, cols],
                                start=True, stop=True)
            banks[r, h] = bank
            tag = "staging1" if (r, h) == (1, 0) else f"least{r}{h}"
            low = sb.tile([P, 1], F32, name=f"least{r}{h}", tag=tag, align_bytes=64)
            nc.vector.tensor_scalar(neg_a[r][:, cols], bank[:], -1.0, least[r][:] if h else None,
                                    ALU.mult, ALU.min, accum_out=low[:])
            least[r] = low

        def weights(r):
            prob[r] = sb.tile([P, I], F32, name=f"p{r}", align_bytes=64)
            z = sb.tile([P, 1], F32, name=f"z{r}")
            nc.scalar.activation(prob[r][:], neg_a[r][:], ACT.Exp, bias=least[r][:], scale=-1.0, accum_out=z[:])
            inv_z[r] = sb.tile([P, 1], F32, name=f"inv_z{r}")
            nc.vector.reciprocal(inv_z[r][:], z[:])

        def weighted_sum(r, h):
            if h == 0:
                sums[r] = sb.tile([P, HALVES], F32, name=f"sums{r}")
            cols = slice(h * BANK, (h + 1) * BANK)
            nc.vector.scalar_tensor_tensor(prob[r][:, cols], banks[r, h][:], -1.0, prob[r][:, cols],
                                           ALU.mult, ALU.mult, accum_out=sums[r][:, h:h + 1])

        def mean(r):
            neg_mean[r] = sb.tile([P, 1], F32, name=f"neg_mean{r}")
            nc.vector.tensor_scalar(neg_mean[r][:], sums[r][:, 0:1], sums[r][:, 1:2], inv_z[r][:],
                                    ALU.add, ALU.mult)

        def distance(r, cols):
            nc.scalar.activation(y[:, r, cols], neg_a[r][:, cols], ACT.Abs, bias=neg_mean[r][:], scale=-1.0)

        def store(rows, cols):
            nc.sync.dma_start(out_rows[:, rows, cols], y[:, rows, cols])

        halves = [slice(h * BANK, (h + 1) * BANK) for h in range(HALVES)]

        def distances(r):
            for cols in halves:
                distance(r, cols)
                store(r, cols)

        scores(0, 0)
        scores(0, 1)
        weights(0)
        scores(1, 0)
        scores(2, 0)
        scores(1, 1)
        weights(1)
        scores(2, 1)
        weights(2)
        weighted_sum(0, 0)
        weighted_sum(0, 1)
        scores(3, 0)
        mean(0)
        distances(0)
        weighted_sum(1, 0)
        scores(3, 1)
        weights(3)
        weighted_sum(1, 1)
        weighted_sum(2, 0)
        mean(1)
        distances(1)
        weighted_sum(2, 1)
        weighted_sum(3, 0)
        mean(2)
        weighted_sum(3, 1)
        mean(3)

        y_codes = sb.tile([P, I], U32, name="y_codes", align_bytes=64)
        y_scales = sb.tile([P, I], U8, name="y_scales", align_bytes=64)
        words_out = out_1[0].rearrange("p c r -> p (c r)").bitcast(I32)
        quarters = [slice(c * QUARTER, (c + 1) * QUARTER) for c in range(I // QUARTER)]
        for r, c in ((2, 0), (2, 1), (2, 2), (3, 0), (3, 1), (2, 3), (3, 2), (3, 3)):
            distance(r, quarters[c])
            if c % 2:
                store(r, halves[c // 2])
        woven = {}

        def weave(c):
            woven[c] = sb.tile([P, QUARTER, PACK], BF16, name=f"woven{c}", align_bytes=64)
            source = y[:, :, quarters[c]].rearrange("p r (c i) -> p c r i", i=2)
            target = woven[c][:].rearrange("p (c i) r -> p c r i", i=2)
            split = min(max(VECTOR_WEAVE - c * QUARTER, 0), QUARTER) // 2
            if split > 0:
                nc.vector.tensor_copy(target[:, :split], source[:, :split])
            if split < QUARTER // 2:
                nc.scalar.copy(target[:, split:], source[:, split:])

        def quantise(c):
            cols = quarters[c]
            nc.vector.quantize_mx(y_codes[:, cols].bitcast(FP8X4), y_scales[:, cols],
                                  woven[c][:].rearrange("p c r -> p (c r)"))
            nc.sync.dma_start(words_out[:, cols], y_codes[:, cols].bitcast(I32))

        weave(0)
        for c in range(len(quarters)):
            if c + 1 < len(quarters):
                weave(c + 1)
            quantise(c)

        for quad in range(4):
            engine = nc.scalar if quad % 2 == 0 else nc.sync
            engine.dma_start(out_2[0, 4 * quad:4 * quad + 4, :].bitcast(I32),
                             y_scales[32 * quad:32 * quad + 4, :].bitcast(I32))
